import numpy as np
import ml_dtypes


def mxq(x, axis, fmt="e4m3"):
    dtype, down = {"e4m3": (ml_dtypes.float8_e4m3fn, 7), "e5m2": (ml_dtypes.float8_e5m2, 14)}[fmt]
    v = np.moveaxis(np.asarray(x, np.float32).astype(ml_dtypes.bfloat16).astype(np.float64), axis, -1)
    blocks = v.reshape(v.shape[:-1] + (-1, 32))
    amax = np.abs(blocks).max(-1, keepdims=True)
    byte = np.maximum(np.where(amax > 0, np.frexp(amax)[1] - 1 + 127, 0) - down, 1)
    scale = np.exp2(byte - 127.0)
    codes = (blocks / scale).astype(np.float32).astype(dtype).astype(np.float64)
    return np.moveaxis((codes * scale).reshape(v.shape), -1, axis)


WIDE = False


def mx_kscale(k):
    if not WIDE:
        return np.ones(k)
    levels = np.array([10, -10, 5, -5, 0])
    if k % 512:
        return np.exp2(np.random.permutation(np.resize(levels, k // 32))).repeat(32)
    a = np.empty((k // 512, 16))
    for p in range(k // 512):
        a[p, :8] = np.random.permutation(np.resize(levels, 8))
        for g in range(8):
            far = levels[np.abs(levels - a[p, g]) >= 10]
            a[p, g + 8] = far[np.random.randint(len(far))]
    return np.exp2(a.ravel()).repeat(32)


def f64(x):
    return np.asarray(x).astype(np.float64)


def striped8(idx):
    return np.asarray(idx).reshape(8, -1, 16).transpose(0, 2, 1).reshape(128, -1).astype(np.uint16)


def unstriped8(offs):
    return offs.reshape(8, 16, -1).transpose(0, 2, 1).reshape(8, -1).astype(np.int64)


def pick8(x, idx, run):
    r = np.arange(len(x))
    return x[r[:, None], idx[r % (8 * run) // run]]


E2M1 = np.array([0.0, 0.5, 1.0, 1.5, 2.0, 3.0, 4.0, 6.0, -0.0, -0.5, -1.0, -1.5, -2.0, -3.0, -4.0, -6.0])


def pack_weight(w, fmt):
    k, n = w.shape
    w = f64(np.asarray(w, np.float32).astype(ml_dtypes.bfloat16)).reshape(k // 32, 32, n)
    amax = np.abs(w).max(1)
    if fmt == "e4m3":
        byte = np.frexp(amax)[1] - 1 + 127 - 7
    else:
        mant, ex = np.frexp(amax / 6.0)
        byte = np.where(mant > 0.5, ex, ex - 1) + 127
    byte = np.clip(np.where(amax > 0, byte, 1), 1, 254)
    scaled = (w * np.exp2(127.0 - byte)[:, None, :]).reshape(k, n).astype(np.float32)
    by_word = np.ascontiguousarray(scaled.reshape(k // 512, 128, 4, n).transpose(0, 1, 3, 2))
    if fmt == "e4m3":
        words = by_word.astype(ml_dtypes.float8_e4m3fn).view(np.uint8)
    else:
        c = by_word.astype(ml_dtypes.float4_e2m1fn).view(np.uint8) & 0xF
        words = (c[..., 0::2] | (c[..., 1::2] << 4)).reshape(k // 512, 128, 2 * n)
    return np.ascontiguousarray(words), np.ascontiguousarray(byte.astype(np.uint8).reshape(k // 512, 16, n))


def unpack_weight(words, scales, fmt):
    g, _, n = scales.shape
    words = np.ascontiguousarray(words).reshape(g, 128, n, -1)
    if fmt == "e4m3":
        vals = words.view(ml_dtypes.float8_e4m3fn).astype(np.float64)
    else:
        nib = np.empty((g, 128, n, 4), np.uint8)
        nib[..., 0::2] = words & 0xF
        nib[..., 1::2] = words >> 4
        vals = E2M1[nib]
    vals = vals * np.repeat(np.exp2(scales.astype(np.float64) - 127.0), 8, axis=1)[..., None]
    return vals.transpose(0, 1, 3, 2).reshape(g * 512, n)


D, T, I, Q = 512, 1024, 512, 128


def setup_inputs():
    n = np.random.standard_normal
    idx = np.stack([np.random.permutation(T)[:I] for _ in range(8)])
    idx2 = np.stack([np.random.permutation(T)[:I] for _ in range(8)])
    idx3 = np.stack([np.random.permutation(T)[:I] for _ in range(8)])
    fd = mx_kscale(D)
    keysp = pack_weight(n((D, T)) / fd[:, None], "e2m1")
    return {
        "query": (n((D, Q)) * 1.2 / np.sqrt(D) * fd[:, None]).astype(np.float32),
        "keys_words": keysp[0],
        "keys_scales": keysp[1],
        "lam": (np.random.uniform(0.8, 1.8, (Q, 1))).astype(np.float32),
        "lean": (np.random.uniform(0.2, 0.6, (Q, 1))).astype(np.float32),
        "base": (0.3 * n((Q, I))).astype(np.float32),
        "gain2": (np.random.uniform(0.5, 2.0, (Q, 1))).astype(np.float32),
        "offs": striped8(idx),
        "offs2": striped8(idx2),
        "offs3": striped8(idx3),
    }


def reference(query, keys_words, keys_scales, lam, lean, base, gain2, offs, offs2, offs3):
    idx = unstriped8(offs)
    idx2 = unstriped8(offs2)
    idx3 = unstriped8(offs3)
    keysu = unpack_weight(keys_words, keys_scales, "e2m1")
    queryq = mxq(f64(query), 0, "e4m3")
    a = queryq.T @ keysu
    lo2 = np.minimum(pick8(a, idx, 16), pick8(a, idx2, 16))
    hi2 = np.maximum(pick8(a, idx, 16), pick8(a, idx2, 16))
    s = np.maximum(lo2, np.minimum(hi2, pick8(a, idx3, 16))) * f64(lam)
    p = np.exp(s - np.max(s, axis=1, keepdims=True))
    r = p / np.sum(p, axis=1, keepdims=True)
    m0 = np.sum(r * s, axis=1, keepdims=True)
    w = r * ((s - m0) * f64(lean) + 1.0)
    y = np.tanh(w * f64(gain2) * 128.0) + f64(base)
    return y

@@ -1,0 +1,158 @@
+from contextlib import ExitStack
+
+import concourse.mybir as mybir
+
+D, T, I, Q = 512, 1024, 512, 128
+FLOPS = 2 * D * Q * T
+
+F32 = mybir.dt.float32
+BF16 = mybir.dt.bfloat16
+I32 = mybir.dt.int32
+U32 = mybir.dt.uint32
+U16 = mybir.dt.uint16
+U8 = mybir.dt.uint8
+FP8X4 = mybir.dt.float8_e4m3fn_x4
+FP4X4 = mybir.dt.float4_e2m1fn_x4
+ALU = mybir.AluOpType
+ACT = mybir.ActivationFunctionType
+
+P = 128
+PACK = 4
+N_MM = 256
+HALF = I // 2
+N_OUT = 128
+
+
+def tile_attend_middle_leaning_gated_heads_kernel(
+    tc, query, keys_words, keys_scales, lam, lean, base, gain2, offs, offs2, offs3, out
+):
+    nc = tc.nc
+    with ExitStack() as ctx:
+        lists = ctx.enter_context(tc.tile_pool(name="lists", bufs=1))
+        sb = ctx.enter_context(tc.tile_pool(name="sb", bufs=1))
+        psum = ctx.enter_context(tc.psum_pool(name="psum", bufs=1))
+
+        k_scale = sb.tile([P, T], U8, align_bytes=64)
+        nc.vector.memset(k_scale[:].bitcast(I32), 0)
+
+        q_raw = sb.tile([P, PACK, Q], F32, tag="stage")
+        nc.sync.dma_start(out=q_raw[:], in_=query.rearrange("(p j) q -> p j q", j=PACK))
+        k_words = sb.tile([P, 2 * T], U8, align_bytes=64)
+        nc.sync.dma_start(out=k_words[:].bitcast(I32), in_=keys_words[0].bitcast(I32))
+        for quad in range(4):
+            nc.sync.dma_start(
+                out=k_scale[32 * quad : 32 * quad + 4, :].bitcast(I32),
+                in_=keys_scales[0][4 * quad : 4 * quad + 4, :].bitcast(I32),
+            )
+        list1 = lists.tile([P, I // 16], U16)
+        list2 = lists.tile([P, I // 16], U16)
+        list3 = lists.tile([P, I // 16], U16)
+        nc.sync.dma_start(list1[:], offs)
+        nc.sync.dma_start(list2[:], offs2)
+        nc.sync.dma_start(list3[:], offs3)
+
+        lam_t = sb.tile([P, 1], F32)
+        lean_t = sb.tile([P, 1], F32)
+        gain_t = sb.tile([P, 1], F32)
+        nc.gpsimd.dma_start(out=lam_t[:], in_=lam)
+        nc.gpsimd.dma_start(out=lean_t[:], in_=lean)
+        nc.gpsimd.dma_start(out=gain_t[:], in_=gain2)
+
+        q_bf = sb.tile([P, Q, PACK], BF16, align_bytes=64)
+        nc.vector.tensor_copy(out=q_bf[:], in_=q_raw[:].rearrange("p j q -> p q j"))
+        q_codes = sb.tile([P, Q], U32, align_bytes=64)
+        q_scale = sb.tile([P, Q], U8, align_bytes=64)
+        nc.vector.quantize_mx(
+            out=q_codes[:].bitcast(FP8X4), scales=q_scale[:], in_=q_bf[:].rearrange("p q j -> p (q j)")
+        )
+
+        base_t = sb.tile([P, I], F32, tag="stage")
+        nc.sync.dma_start(out=base_t[:], in_=base)
+
+        neg_lam = sb.tile([P, 1], F32)
+        nc.scalar.activation(out=neg_lam[:], in_=lam_t[:], func=ACT.Copy, scale=-1.0)
+
+        scores = sb.tile([P, T], F32)
+        for b in range(T // N_MM):
+            bank = psum.tile([P, N_MM], F32, name=f"bank{b}")
+            nc.tensor.matmul_mx(
+                out=bank[:],
+                lhsT=q_codes[:].bitcast(FP8X4),
+                lhsT_scale=q_scale[:],
+                rhs=k_words[:, 2 * b * N_MM : 2 * (b + 1) * N_MM].bitcast(FP4X4),
+                rhs_scale=k_scale[:, b * N_MM : (b + 1) * N_MM],
+                start=True,
+                stop=True,
+            )
+            cols = scores[:, b * N_MM : (b + 1) * N_MM]
+            if b % 2 == 0:
+                nc.scalar.copy(out=cols, in_=bank[:])
+            else:
+                nc.vector.tensor_copy(out=cols, in_=bank[:])
+
+        def half_tiles(name):
+            return [sb.tile([P, HALF], F32, name=f"{name}{h}") for h in range(2)]
+
+        def picked(lst, h):
+            return scores[:].indirect(lst[:, h * HALF // 16 : (h + 1) * HALF // 16])
+
+        g1, g2, g3 = half_tiles("g1_"), half_tiles("g2_"), half_tiles("g3_")
+        hi, lo, low_hi, mid = half_tiles("hi"), half_tiles("lo"), half_tiles("low_hi"), half_tiles("mid")
+        for h in range(2):
+            nc.vector.tensor_copy(out=g1[h][:], in_=picked(list1, h))
+            nc.scalar.activation(out=g2[h][:], in_=picked(list2, h), func=ACT.Copy)
+        for h in range(2):
+            nc.scalar.activation(out=g3[h][:], in_=picked(list3, h), func=ACT.Copy)
+        for h in range(2):
+            nc.vector.tensor_tensor(out=hi[h][:], in0=g1[h][:], in1=g2[h][:], op=ALU.max)
+            nc.vector.tensor_tensor(out=lo[h][:], in0=g1[h][:], in1=g2[h][:], op=ALU.min)
+        for h in range(2):
+            nc.vector.tensor_tensor(out=low_hi[h][:], in0=hi[h][:], in1=g3[h][:], op=ALU.min)
+        for h in range(2):
+            nc.vector.tensor_tensor(out=mid[h][:], in0=lo[h][:], in1=low_hi[h][:], op=ALU.max)
+
+        neg_s = sb.tile([P, I], F32)
+        neg_max0 = sb.tile([P, 1], F32)
+        neg_max = sb.tile([P, 1], F32)
+        nc.vector.tensor_scalar(
+            out=neg_s[:, :HALF], in0=mid[0][:], scalar1=neg_lam[:], scalar2=None,
+            op0=ALU.mult, op1=ALU.min, accum_out=neg_max0[:],
+        )
+        nc.vector.tensor_scalar(
+            out=neg_s[:, HALF:], in0=mid[1][:], scalar1=neg_lam[:], scalar2=neg_max0[:],
+            op0=ALU.mult, op1=ALU.min, accum_out=neg_max[:],
+        )
+
+        p = sb.tile([P, I], F32)
+        p_sum = sb.tile([P, 1], F32)
+        nc.scalar.activation(out=p[:], in_=neg_s[:], func=ACT.Exp, scale=-1.0, bias=neg_max[:], accum_out=p_sum[:])
+        inv_sum = sb.tile([P, 1], F32)
+        nc.vector.reciprocal(out=inv_sum[:], in_=p_sum[:])
+        neg_e = sb.tile([P, I], F32)
+        neg_e_sum = sb.tile([P, 1], F32)
+        nc.vector.scalar_tensor_tensor(
+            out=neg_e[:], in0=neg_s[:], scalar=lean_t[:], in1=p[:], op0=ALU.mult, op1=ALU.mult, accum_out=neg_e_sum[:]
+        )
+        tanh_scale = sb.tile([P, 1], F32)
+        nc.vector.tensor_scalar(
+            out=tanh_scale[:], in0=inv_sum[:], scalar1=gain_t[:], scalar2=128.0, op0=ALU.mult, op1=ALU.mult
+        )
+        p_factor = sb.tile([P, 1], F32)
+        nc.vector.tensor_scalar(
+            out=p_factor[:], in0=neg_e_sum[:], scalar1=inv_sum[:], scalar2=1.0, op0=ALU.mult, op1=ALU.add
+        )
+
+        pieces = [slice(c, c + N_OUT) for c in range(0, I, N_OUT)]
+        w = [sb.tile([P, N_OUT], F32, name=f"w{c}") for c in range(len(pieces))]
+        gated = [sb.tile([P, N_OUT], F32, name=f"gated{c}") for c in range(len(pieces))]
+        y = sb.tile([P, I], F32)
+        for c, cols in enumerate(pieces):
+            nc.vector.scalar_tensor_tensor(
+                out=w[c][:], in0=p[:, cols], scalar=p_factor[:], in1=neg_e[:, cols], op0=ALU.mult, op1=ALU.subtract
+            )
+            nc.scalar.activation(out=gated[c][:], in_=w[c][:], func=ACT.Tanh, scale=tanh_scale[:])
+        for c, cols in enumerate(pieces):
+            nc.vector.tensor_tensor(out=y[:, cols], in0=gated[c][:], in1=base_t[:, cols], op=ALU.add)
+        for h in range(2):
+            cols = slice(h * HALF, (h + 1) * HALF)
+            nc.sync.dma_start(out=out[:, cols], in_=y[:, cols])

@@ -18,8 +18,9 @@ ACT = mybir.ActivationFunctionType
 
 P = 128
 PACK = 4
-N_MM = 256
+MM_WIDTHS = (256, 256, 256, 128, 128)
 HALF = I // 2
+CAST_SPLIT = 16
 N_OUT = 128
 
 
@@ -37,13 +38,14 @@ def tile_attend_middle_leaning_gated_heads_kernel(
 
         q_raw = sb.tile([P, PACK, Q], F32, tag="stage")
         nc.sync.dma_start(out=q_raw[:], in_=query.rearrange("(p j) q -> p j q", j=PACK))
-        k_words = sb.tile([P, 2 * T], U8, align_bytes=64)
-        nc.sync.dma_start(out=k_words[:].bitcast(I32), in_=keys_words[0].bitcast(I32))
+        k_words = [sb.tile([P, T], U8, name=f"k_words{i}", align_bytes=64) for i in range(2)]
+        nc.sync.dma_start(out=k_words[0][:].bitcast(I32), in_=keys_words[0][:, :T].bitcast(I32))
         for quad in range(4):
             nc.sync.dma_start(
                 out=k_scale[32 * quad : 32 * quad + 4, :].bitcast(I32),
                 in_=keys_scales[0][4 * quad : 4 * quad + 4, :].bitcast(I32),
             )
+        nc.sync.dma_start(out=k_words[1][:].bitcast(I32), in_=keys_words[0][:, T:].bitcast(I32))
         list1 = lists.tile([P, I // 16], U16)
         list2 = lists.tile([P, I // 16], U16)
         list3 = lists.tile([P, I // 16], U16)
@@ -54,12 +56,15 @@ def tile_attend_middle_leaning_gated_heads_kernel(
         lam_t = sb.tile([P, 1], F32)
         lean_t = sb.tile([P, 1], F32)
         gain_t = sb.tile([P, 1], F32)
-        nc.gpsimd.dma_start(out=lam_t[:], in_=lam)
-        nc.gpsimd.dma_start(out=lean_t[:], in_=lean)
-        nc.gpsimd.dma_start(out=gain_t[:], in_=gain2)
+        nc.sync.dma_start(out=lam_t[:], in_=lam)
+        nc.sync.dma_start(out=lean_t[:], in_=lean)
+        nc.sync.dma_start(out=gain_t[:], in_=gain2)
 
         q_bf = sb.tile([P, Q, PACK], BF16, align_bytes=64)
-        nc.vector.tensor_copy(out=q_bf[:], in_=q_raw[:].rearrange("p j q -> p q j"))
+        q_dst = q_bf[:].rearrange("p (c i) j -> p c j i", i=4)
+        q_src = q_raw[:].rearrange("p j (c i) -> p c j i", i=4)
+        nc.vector.tensor_copy(out=q_dst[:, :CAST_SPLIT], in_=q_src[:, :CAST_SPLIT])
+        nc.scalar.activation(out=q_dst[:, CAST_SPLIT:], in_=q_src[:, CAST_SPLIT:], func=ACT.Copy)
         q_codes = sb.tile([P, Q], U32, align_bytes=64)
         q_scale = sb.tile([P, Q], U8, align_bytes=64)
         nc.vector.quantize_mx(
@@ -69,26 +74,26 @@ def tile_attend_middle_leaning_gated_heads_kernel(
         base_t = sb.tile([P, I], F32, tag="stage")
         nc.sync.dma_start(out=base_t[:], in_=base)
 
-        neg_lam = sb.tile([P, 1], F32)
-        nc.scalar.activation(out=neg_lam[:], in_=lam_t[:], func=ACT.Copy, scale=-1.0)
-
         scores = sb.tile([P, T], F32)
-        for b in range(T // N_MM):
-            bank = psum.tile([P, N_MM], F32, name=f"bank{b}")
+        t0 = 0
+        for b, width in enumerate(MM_WIDTHS):
+            bank = psum.tile([P, width], F32, name=f"bank{b}")
+            part, first = divmod(t0, T // 2)
             nc.tensor.matmul_mx(
                 out=bank[:],
                 lhsT=q_codes[:].bitcast(FP8X4),
                 lhsT_scale=q_scale[:],
-                rhs=k_words[:, 2 * b * N_MM : 2 * (b + 1) * N_MM].bitcast(FP4X4),
-                rhs_scale=k_scale[:, b * N_MM : (b + 1) * N_MM],
+                rhs=k_words[part][:, 2 * first : 2 * (first + width)].bitcast(FP4X4),
+                rhs_scale=k_scale[:, t0 : t0 + width],
                 start=True,
                 stop=True,
             )
-            cols = scores[:, b * N_MM : (b + 1) * N_MM]
+            cols = scores[:, t0 : t0 + width]
             if b % 2 == 0:
-                nc.scalar.copy(out=cols, in_=bank[:])
+                nc.scalar.activation(out=cols, in_=bank[:], func=ACT.Copy)
             else:
                 nc.vector.tensor_copy(out=cols, in_=bank[:])
+            t0 = t0 + width
 
         def half_tiles(name):
             return [sb.tile([P, HALF], F32, name=f"{name}{h}") for h in range(2)]
@@ -98,61 +103,94 @@ def tile_attend_middle_leaning_gated_heads_kernel(
 
         g1, g2, g3 = half_tiles("g1_"), half_tiles("g2_"), half_tiles("g3_")
         hi, lo, low_hi, mid = half_tiles("hi"), half_tiles("lo"), half_tiles("low_hi"), half_tiles("mid")
+        neg_s, p, neg_e = half_tiles("neg_s"), half_tiles("p"), half_tiles("neg_e")
+        neg_max = [sb.tile([P, 1], F32, name=f"neg_max{h}") for h in range(2)]
+        p_sum = [sb.tile([P, 1], F32, name=f"p_sum{h}") for h in range(2)]
+        neg_e_sum0 = sb.tile([P, 1], F32)
+        neg_e_sums = sb.tile([P, 2], F32)
+        gains = sb.tile([P, 2], F32)
+        neg_lam = sb.tile([P, 1], F32)
+
         for h in range(2):
             nc.vector.tensor_copy(out=g1[h][:], in_=picked(list1, h))
+        for h in range(2):
             nc.scalar.activation(out=g2[h][:], in_=picked(list2, h), func=ACT.Copy)
-        for h in range(2):
             nc.scalar.activation(out=g3[h][:], in_=picked(list3, h), func=ACT.Copy)
-        for h in range(2):
+        nc.scalar.activation(out=neg_lam[:], in_=lam_t[:], func=ACT.Copy, scale=-1.0)
+        nc.scalar.activation(out=gains[:, 1:2], in_=gain_t[:], func=ACT.Copy, scale=128.0)
+
+        def pair_max(h):
             nc.vector.tensor_tensor(out=hi[h][:], in0=g1[h][:], in1=g2[h][:], op=ALU.max)
+
+        def pair_min(h):
             nc.vector.tensor_tensor(out=lo[h][:], in0=g1[h][:], in1=g2[h][:], op=ALU.min)
-        for h in range(2):
+
+        def cap_third(h):
             nc.vector.tensor_tensor(out=low_hi[h][:], in0=hi[h][:], in1=g3[h][:], op=ALU.min)
-        for h in range(2):
+
+        def median(h):
             nc.vector.tensor_tensor(out=mid[h][:], in0=lo[h][:], in1=low_hi[h][:], op=ALU.max)
 
-        neg_s = sb.tile([P, I], F32)
-        neg_max0 = sb.tile([P, 1], F32)
-        neg_max = sb.tile([P, 1], F32)
-        nc.vector.tensor_scalar(
-            out=neg_s[:, :HALF], in0=mid[0][:], scalar1=neg_lam[:], scalar2=None,
-            op0=ALU.mult, op1=ALU.min, accum_out=neg_max0[:],
-        )
-        nc.vector.tensor_scalar(
-            out=neg_s[:, HALF:], in0=mid[1][:], scalar1=neg_lam[:], scalar2=neg_max0[:],
-            op0=ALU.mult, op1=ALU.min, accum_out=neg_max[:],
-        )
+        def scale_and_max(h, start):
+            nc.vector.tensor_scalar(
+                out=neg_s[h][:], in0=mid[h][:], scalar1=neg_lam[:], scalar2=start,
+                op0=ALU.mult, op1=ALU.min, accum_out=neg_max[h][:],
+            )
 
-        p = sb.tile([P, I], F32)
-        p_sum = sb.tile([P, 1], F32)
-        nc.scalar.activation(out=p[:], in_=neg_s[:], func=ACT.Exp, scale=-1.0, bias=neg_max[:], accum_out=p_sum[:])
-        inv_sum = sb.tile([P, 1], F32)
-        nc.vector.reciprocal(out=inv_sum[:], in_=p_sum[:])
-        neg_e = sb.tile([P, I], F32)
-        neg_e_sum = sb.tile([P, 1], F32)
-        nc.vector.scalar_tensor_tensor(
-            out=neg_e[:], in0=neg_s[:], scalar=lean_t[:], in1=p[:], op0=ALU.mult, op1=ALU.mult, accum_out=neg_e_sum[:]
-        )
-        tanh_scale = sb.tile([P, 1], F32)
-        nc.vector.tensor_scalar(
-            out=tanh_scale[:], in0=inv_sum[:], scalar1=gain_t[:], scalar2=128.0, op0=ALU.mult, op1=ALU.mult
-        )
+        def exp_and_sum(h):
+            nc.scalar.activation(
+                out=p[h][:], in_=neg_s[h][:], func=ACT.Exp, scale=-1.0, bias=neg_max[h][:], accum_out=p_sum[h][:]
+            )
+
+        def lean_and_sum(h, total):
+            nc.vector.scalar_tensor_tensor(
+                out=neg_e[h][:], in0=neg_s[h][:], scalar=lean_t[:], in1=p[h][:],
+                op0=ALU.mult, op1=ALU.mult, accum_out=total,
+            )
+
+        pair_max(0)
+        pair_min(0)
+        cap_third(0)
+        pair_max(1)
+        median(0)
+        pair_min(1)
+        cap_third(1)
+        scale_and_max(0, None)
+        exp_and_sum(0)
+        median(1)
+        scale_and_max(1, neg_max[0][:])
+        rescale = sb.tile([P, 1], F32)
+        nc.scalar.activation(out=rescale[:], in_=neg_max[0][:], func=ACT.Exp, scale=-1.0, bias=neg_max[1][:])
+        exp_and_sum(1)
+        lean_and_sum(0, neg_e_sum0[:])
+        total = sb.tile([P, 1], F32)
+        nc.scalar.activation(out=total[:], in_=p_sum[0][:], func=ACT.Identity, scale=rescale[:], bias=p_sum[1][:])
+        nc.scalar.activation(out=neg_e_sums[:, 0:1], in_=neg_e_sum0[:], func=ACT.Copy, scale=rescale[:])
+        nc.scalar.activation(out=gains[:, 0:1], in_=gains[:, 1:2], func=ACT.Copy, scale=rescale[:])
+        lean_and_sum(1, neg_e_sums[:, 1:2])
+        inv_total = sb.tile([P, 1], F32)
+        nc.vector.reciprocal(out=inv_total[:], in_=total[:])
+        neg_means = sb.tile([P, 2], F32)
         p_factor = sb.tile([P, 1], F32)
         nc.vector.tensor_scalar(
-            out=p_factor[:], in0=neg_e_sum[:], scalar1=inv_sum[:], scalar2=1.0, op0=ALU.mult, op1=ALU.add
+            out=neg_means[:], in0=neg_e_sums[:], scalar1=inv_total[:], scalar2=1.0,
+            op0=ALU.mult, op1=ALU.add, accum_out=p_factor[:],
         )
+        tanh_scale = sb.tile([P, 2], F32)
+        nc.scalar.activation(out=tanh_scale[:], in_=gains[:], func=ACT.Copy, scale=inv_total[:])
 
         pieces = [slice(c, c + N_OUT) for c in range(0, I, N_OUT)]
         w = [sb.tile([P, N_OUT], F32, name=f"w{c}") for c in range(len(pieces))]
         gated = [sb.tile([P, N_OUT], F32, name=f"gated{c}") for c in range(len(pieces))]
         y = sb.tile([P, I], F32)
         for c, cols in enumerate(pieces):
+            h, first = divmod(cols.start, HALF)
+            part = slice(first, first + N_OUT)
             nc.vector.scalar_tensor_tensor(
-                out=w[c][:], in0=p[:, cols], scalar=p_factor[:], in1=neg_e[:, cols], op0=ALU.mult, op1=ALU.subtract
+                out=w[c][:], in0=p[h][:, part], scalar=p_factor[:], in1=neg_e[h][:, part],
+                op0=ALU.mult, op1=ALU.subtract,
             )
-            nc.scalar.activation(out=gated[c][:], in_=w[c][:], func=ACT.Tanh, scale=tanh_scale[:])
+            nc.scalar.activation(out=gated[c][:], in_=w[c][:], func=ACT.Tanh, scale=tanh_scale[:, h : h + 1])
         for c, cols in enumerate(pieces):
             nc.vector.tensor_tensor(out=y[:, cols], in0=gated[c][:], in1=base_t[:, cols], op=ALU.add)
-        for h in range(2):
-            cols = slice(h * HALF, (h + 1) * HALF)
             nc.sync.dma_start(out=out[:, cols], in_=y[:, cols])

from contextlib import ExitStack

import concourse.mybir as mybir

D, T, I, Q = 512, 1024, 512, 128
FLOPS = 2 * D * Q * T

F32 = mybir.dt.float32
BF16 = mybir.dt.bfloat16
I32 = mybir.dt.int32
U32 = mybir.dt.uint32
U16 = mybir.dt.uint16
U8 = mybir.dt.uint8
FP8X4 = mybir.dt.float8_e4m3fn_x4
FP4X4 = mybir.dt.float4_e2m1fn_x4
ALU = mybir.AluOpType
ACT = mybir.ActivationFunctionType

P = 128
PACK = 4
MM_WIDTHS = (256, 256, 256, 128, 128)
HALF = I // 2
CAST_SPLIT = 16
N_OUT = 128


def tile_attend_middle_leaning_gated_heads_kernel(
    tc, query, keys_words, keys_scales, lam, lean, base, gain2, offs, offs2, offs3, out
):
    nc = tc.nc
    with ExitStack() as ctx:
        lists = ctx.enter_context(tc.tile_pool(name="lists", bufs=1))
        sb = ctx.enter_context(tc.tile_pool(name="sb", bufs=1))
        psum = ctx.enter_context(tc.psum_pool(name="psum", bufs=1))

        k_scale = sb.tile([P, T], U8, align_bytes=64)
        nc.vector.memset(k_scale[:].bitcast(I32), 0)

        q_raw = sb.tile([P, PACK, Q], F32, tag="stage")
        nc.sync.dma_start(out=q_raw[:], in_=query.rearrange("(p j) q -> p j q", j=PACK))
        k_words = [sb.tile([P, T], U8, name=f"k_words{i}", align_bytes=64) for i in range(2)]
        nc.sync.dma_start(out=k_words[0][:].bitcast(I32), in_=keys_words[0][:, :T].bitcast(I32))
        for quad in range(4):
            nc.sync.dma_start(
                out=k_scale[32 * quad : 32 * quad + 4, :].bitcast(I32),
                in_=keys_scales[0][4 * quad : 4 * quad + 4, :].bitcast(I32),
            )
        nc.sync.dma_start(out=k_words[1][:].bitcast(I32), in_=keys_words[0][:, T:].bitcast(I32))
        list1 = lists.tile([P, I // 16], U16)
        list2 = lists.tile([P, I // 16], U16)
        list3 = lists.tile([P, I // 16], U16)
        nc.sync.dma_start(list1[:], offs)
        nc.sync.dma_start(list2[:], offs2)
        nc.sync.dma_start(list3[:], offs3)

        lam_t = sb.tile([P, 1], F32)
        lean_t = sb.tile([P, 1], F32)
        gain_t = sb.tile([P, 1], F32)
        nc.sync.dma_start(out=lam_t[:], in_=lam)
        nc.sync.dma_start(out=lean_t[:], in_=lean)
        nc.sync.dma_start(out=gain_t[:], in_=gain2)

        q_bf = sb.tile([P, Q, PACK], BF16, align_bytes=64)
        q_dst = q_bf[:].rearrange("p (c i) j -> p c j i", i=4)
        q_src = q_raw[:].rearrange("p j (c i) -> p c j i", i=4)
        nc.vector.tensor_copy(out=q_dst[:, :CAST_SPLIT], in_=q_src[:, :CAST_SPLIT])
        nc.scalar.activation(out=q_dst[:, CAST_SPLIT:], in_=q_src[:, CAST_SPLIT:], func=ACT.Copy)
        q_codes = sb.tile([P, Q], U32, align_bytes=64)
        q_scale = sb.tile([P, Q], U8, align_bytes=64)
        nc.vector.quantize_mx(
            out=q_codes[:].bitcast(FP8X4), scales=q_scale[:], in_=q_bf[:].rearrange("p q j -> p (q j)")
        )

        base_t = sb.tile([P, I], F32, tag="stage")
        nc.sync.dma_start(out=base_t[:], in_=base)

        scores = sb.tile([P, T], F32)
        t0 = 0
        for b, width in enumerate(MM_WIDTHS):
            bank = psum.tile([P, width], F32, name=f"bank{b}")
            part, first = divmod(t0, T // 2)
            nc.tensor.matmul_mx(
                out=bank[:],
                lhsT=q_codes[:].bitcast(FP8X4),
                lhsT_scale=q_scale[:],
                rhs=k_words[part][:, 2 * first : 2 * (first + width)].bitcast(FP4X4),
                rhs_scale=k_scale[:, t0 : t0 + width],
                start=True,
                stop=True,
            )
            cols = scores[:, t0 : t0 + width]
            if b % 2 == 0:
                nc.scalar.activation(out=cols, in_=bank[:], func=ACT.Copy)
            else:
                nc.vector.tensor_copy(out=cols, in_=bank[:])
            t0 = t0 + width

        def half_tiles(name):
            return [sb.tile([P, HALF], F32, name=f"{name}{h}") for h in range(2)]

        def picked(lst, h):
            return scores[:].indirect(lst[:, h * HALF // 16 : (h + 1) * HALF // 16])

        g1, g2, g3 = half_tiles("g1_"), half_tiles("g2_"), half_tiles("g3_")
        hi, lo, low_hi, mid = half_tiles("hi"), half_tiles("lo"), half_tiles("low_hi"), half_tiles("mid")
        neg_s, p, neg_e = half_tiles("neg_s"), half_tiles("p"), half_tiles("neg_e")
        neg_max = [sb.tile([P, 1], F32, name=f"neg_max{h}") for h in range(2)]
        p_sum = [sb.tile([P, 1], F32, name=f"p_sum{h}") for h in range(2)]
        neg_e_sum0 = sb.tile([P, 1], F32)
        neg_e_sums = sb.tile([P, 2], F32)
        gains = sb.tile([P, 2], F32)
        neg_lam = sb.tile([P, 1], F32)

        for h in range(2):
            nc.vector.tensor_copy(out=g1[h][:], in_=picked(list1, h))
        for h in range(2):
            nc.scalar.activation(out=g2[h][:], in_=picked(list2, h), func=ACT.Copy)
            nc.scalar.activation(out=g3[h][:], in_=picked(list3, h), func=ACT.Copy)
        nc.scalar.activation(out=neg_lam[:], in_=lam_t[:], func=ACT.Copy, scale=-1.0)
        nc.scalar.activation(out=gains[:, 1:2], in_=gain_t[:], func=ACT.Copy, scale=128.0)

        def pair_max(h):
            nc.vector.tensor_tensor(out=hi[h][:], in0=g1[h][:], in1=g2[h][:], op=ALU.max)

        def pair_min(h):
            nc.vector.tensor_tensor(out=lo[h][:], in0=g1[h][:], in1=g2[h][:], op=ALU.min)

        def cap_third(h):
            nc.vector.tensor_tensor(out=low_hi[h][:], in0=hi[h][:], in1=g3[h][:], op=ALU.min)

        def median(h):
            nc.vector.tensor_tensor(out=mid[h][:], in0=lo[h][:], in1=low_hi[h][:], op=ALU.max)

        def scale_and_max(h, start):
            nc.vector.tensor_scalar(
                out=neg_s[h][:], in0=mid[h][:], scalar1=neg_lam[:], scalar2=start,
                op0=ALU.mult, op1=ALU.min, accum_out=neg_max[h][:],
            )

        def exp_and_sum(h):
            nc.scalar.activation(
                out=p[h][:], in_=neg_s[h][:], func=ACT.Exp, scale=-1.0, bias=neg_max[h][:], accum_out=p_sum[h][:]
            )

        def lean_and_sum(h, total):
            nc.vector.scalar_tensor_tensor(
                out=neg_e[h][:], in0=neg_s[h][:], scalar=lean_t[:], in1=p[h][:],
                op0=ALU.mult, op1=ALU.mult, accum_out=total,
            )

        pair_max(0)
        pair_min(0)
        cap_third(0)
        pair_max(1)
        median(0)
        pair_min(1)
        cap_third(1)
        scale_and_max(0, None)
        exp_and_sum(0)
        median(1)
        scale_and_max(1, neg_max[0][:])
        rescale = sb.tile([P, 1], F32)
        nc.scalar.activation(out=rescale[:], in_=neg_max[0][:], func=ACT.Exp, scale=-1.0, bias=neg_max[1][:])
        exp_and_sum(1)
        lean_and_sum(0, neg_e_sum0[:])
        total = sb.tile([P, 1], F32)
        nc.scalar.activation(out=total[:], in_=p_sum[0][:], func=ACT.Identity, scale=rescale[:], bias=p_sum[1][:])
        nc.scalar.activation(out=neg_e_sums[:, 0:1], in_=neg_e_sum0[:], func=ACT.Copy, scale=rescale[:])
        nc.scalar.activation(out=gains[:, 0:1], in_=gains[:, 1:2], func=ACT.Copy, scale=rescale[:])
        lean_and_sum(1, neg_e_sums[:, 1:2])
        inv_total = sb.tile([P, 1], F32)
        nc.vector.reciprocal(out=inv_total[:], in_=total[:])
        neg_means = sb.tile([P, 2], F32)
        p_factor = sb.tile([P, 1], F32)
        nc.vector.tensor_scalar(
            out=neg_means[:], in0=neg_e_sums[:], scalar1=inv_total[:], scalar2=1.0,
            op0=ALU.mult, op1=ALU.add, accum_out=p_factor[:],
        )
        tanh_scale = sb.tile([P, 2], F32)
        nc.scalar.activation(out=tanh_scale[:], in_=gains[:], func=ACT.Copy, scale=inv_total[:])

        pieces = [slice(c, c + N_OUT) for c in range(0, I, N_OUT)]
        w = [sb.tile([P, N_OUT], F32, name=f"w{c}") for c in range(len(pieces))]
        gated = [sb.tile([P, N_OUT], F32, name=f"gated{c}") for c in range(len(pieces))]
        y = sb.tile([P, I], F32)
        for c, cols in enumerate(pieces):
            h, first = divmod(cols.start, HALF)
            part = slice(first, first + N_OUT)
            nc.vector.scalar_tensor_tensor(
                out=w[c][:], in0=p[h][:, part], scalar=p_factor[:], in1=neg_e[h][:, part],
                op0=ALU.mult, op1=ALU.subtract,
            )
            nc.scalar.activation(out=gated[c][:], in_=w[c][:], func=ACT.Tanh, scale=tanh_scale[:, h : h + 1])
        for c, cols in enumerate(pieces):
            nc.vector.tensor_tensor(out=y[:, cols], in0=gated[c][:], in1=base_t[:, cols], op=ALU.add)
            nc.sync.dma_start(out=out[:, cols], in_=y[:, cols])
